import numpy as np
import ml_dtypes


def mxq(x, axis, fmt="e4m3"):
    dtype, down = {"e4m3": (ml_dtypes.float8_e4m3fn, 7), "e5m2": (ml_dtypes.float8_e5m2, 14)}[fmt]
    v = np.moveaxis(np.asarray(x, np.float32).astype(ml_dtypes.bfloat16).astype(np.float64), axis, -1)
    blocks = v.reshape(v.shape[:-1] + (-1, 32))
    amax = np.abs(blocks).max(-1, keepdims=True)
    byte = np.maximum(np.where(amax > 0, np.frexp(amax)[1] - 1 + 127, 0) - down, 1)
    scale = np.exp2(byte - 127.0)
    codes = (blocks / scale).astype(np.float32).astype(dtype).astype(np.float64)
    return np.moveaxis((codes * scale).reshape(v.shape), -1, axis)


WIDE = False


def mx_kscale(k):
    if not WIDE:
        return np.ones(k)
    levels = np.array([10, -10, 5, -5, 0])
    if k % 512:
        return np.exp2(np.random.permutation(np.resize(levels, k // 32))).repeat(32)
    a = np.empty((k // 512, 16))
    for p in range(k // 512):
        a[p, :8] = np.random.permutation(np.resize(levels, 8))
        for g in range(8):
            far = levels[np.abs(levels - a[p, g]) >= 10]
            a[p, g + 8] = far[np.random.randint(len(far))]
    return np.exp2(a.ravel()).repeat(32)


def f64(x):
    return np.asarray(x).astype(np.float64)


def striped8(idx):
    return np.asarray(idx).reshape(8, -1, 16).transpose(0, 2, 1).reshape(128, -1).astype(np.uint16)


def unstriped8(offs):
    return offs.reshape(8, 16, -1).transpose(0, 2, 1).reshape(8, -1).astype(np.int64)


def pick8(x, idx, run):
    r = np.arange(len(x))
    return x[r[:, None], idx[r % (8 * run) // run]]


E2M1 = np.array([0.0, 0.5, 1.0, 1.5, 2.0, 3.0, 4.0, 6.0, -0.0, -0.5, -1.0, -1.5, -2.0, -3.0, -4.0, -6.0])


def pack_weight(w, fmt):
    k, n = w.shape
    w = f64(np.asarray(w, np.float32).astype(ml_dtypes.bfloat16)).reshape(k // 32, 32, n)
    amax = np.abs(w).max(1)
    if fmt == "e4m3":
        byte = np.frexp(amax)[1] - 1 + 127 - 7
    else:
        mant, ex = np.frexp(amax / 6.0)
        byte = np.where(mant > 0.5, ex, ex - 1) + 127
    byte = np.clip(np.where(amax > 0, byte, 1), 1, 254)
    scaled = (w * np.exp2(127.0 - byte)[:, None, :]).reshape(k, n).astype(np.float32)
    by_word = np.ascontiguousarray(scaled.reshape(k // 512, 128, 4, n).transpose(0, 1, 3, 2))
    if fmt == "e4m3":
        words = by_word.astype(ml_dtypes.float8_e4m3fn).view(np.uint8)
    else:
        c = by_word.astype(ml_dtypes.float4_e2m1fn).view(np.uint8) & 0xF
        words = (c[..., 0::2] | (c[..., 1::2] << 4)).reshape(k // 512, 128, 2 * n)
    return np.ascontiguousarray(words), np.ascontiguousarray(byte.astype(np.uint8).reshape(k // 512, 16, n))


def unpack_weight(words, scales, fmt):
    g, _, n = scales.shape
    words = np.ascontiguousarray(words).reshape(g, 128, n, -1)
    if fmt == "e4m3":
        vals = words.view(ml_dtypes.float8_e4m3fn).astype(np.float64)
    else:
        nib = np.empty((g, 128, n, 4), np.uint8)
        nib[..., 0::2] = words & 0xF
        nib[..., 1::2] = words >> 4
        vals = E2M1[nib]
    vals = vals * np.repeat(np.exp2(scales.astype(np.float64) - 127.0), 8, axis=1)[..., None]
    return vals.transpose(0, 1, 3, 2).reshape(g * 512, n)


def bf(x):
    return np.asarray(x, np.float32).astype(ml_dtypes.bfloat16)


def planes(Y):
    r, m = Y.shape
    b = f64(bf(Y)).reshape(r // 32, 32, m)
    amax = np.abs(b).max(1)
    byte = np.clip(np.where(amax > 0, np.frexp(amax)[1] - 1 + 127 - 7, 1), 1, 254)
    codes = (b * np.exp2(127.0 - byte)[:, None, :]).reshape(r, m).astype(np.float32).astype(ml_dtypes.float8_e4m3fn).view(np.uint8)
    words = codes.reshape(r // 512, 128, 4, m).transpose(0, 1, 3, 2)
    return np.ascontiguousarray(words), np.ascontiguousarray(byte.astype(np.uint8).reshape(r // 512, 16, m))


K, T, J, C = 512, 1024, 512, 512


def setup_inputs():
    n = np.random.standard_normal
    idx = np.stack([np.random.permutation(T)[:J] for _ in range(8)])
    fk = mx_kscale(K)
    wcp = pack_weight(n((K, C)) * 1 / np.sqrt(K) * fk[:, None], "e2m1")
    return {
        "xt": (n((K, T)) * 0.5 / fk[:, None]).astype(np.float32),
        "wc_words": wcp[0],
        "wc_scales": wcp[1],
        "offs": striped8(idx),
    }


def reference(xt, wc_words, wc_scales, offs):
    idx = unstriped8(offs)
    wcu = unpack_weight(wc_words, wc_scales, "e2m1")
    xtidxq = mxq(pick8(f64(xt), idx, 64), 0, "e4m3")
    a = xtidxq.T @ wcu
    e = np.exp(a)
    y = 256.0 * e / np.sum(e, axis=1, keepdims=True)
    words, scales = planes(y)
    return y, words, scales

@@ -1,0 +1,142 @@
+from contextlib import ExitStack
+
+import concourse.mybir as mybir
+
+K, T, J, C = 512, 1024, 512, 512
+FLOPS = 2 * J * K * C
+
+F32 = mybir.dt.float32
+BF16 = mybir.dt.bfloat16
+I32 = mybir.dt.int32
+U32 = mybir.dt.uint32
+U16 = mybir.dt.uint16
+U8 = mybir.dt.uint8
+FP8X4 = mybir.dt.float8_e4m3fn_x4
+FP4X4 = mybir.dt.float4_e2m1fn_x4
+ALU = mybir.AluOpType
+EXP = mybir.ActivationFunctionType.Exp
+AX = mybir.AxisListType.X
+
+P = 128
+PACK = 4
+
+
+def tile_moe_expert_heads_to_classes_pl_kernel(tc, xt, wc_words, wc_scales, offs, out_0, out_1, out_2):
+    nc = tc.nc
+    with ExitStack() as ctx:
+        sb = ctx.enter_context(tc.tile_pool(name="sb", bufs=1))
+        ps = ctx.enter_context(tc.psum_pool(name="ps", bufs=1))
+
+        offsets = sb.tile([P, J // 16], U16, name="offsets")
+        rows = [sb.tile([P, T], F32, name=f"rows{r}") for r in range(PACK)]
+        w_words = sb.tile([P, 2 * C], U8, name="w_words", align_bytes=64)
+        w_scales = sb.tile([P, C], U8, name="w_scales", align_bytes=64)
+        warm_in = sb.tile([P, 1], F32, name="warm_in")
+        warm_out = sb.tile([P, 1], F32, name="warm_out")
+
+        nc.gpsimd.memset(warm_in[:], 0.0)
+        nc.gpsimd.memset(w_scales[:].bitcast(I32), 0)
+        nc.scalar.activation(warm_out[:], warm_in[:], EXP)
+
+        xt_rows = xt.rearrange("(p r) t -> p r t", r=PACK)
+        nc.sync.dma_start(rows[0][:], xt_rows[:, 0, :])
+        nc.sync.dma_start(offsets[:], offs)
+        for r in range(1, PACK):
+            nc.sync.dma_start(rows[r][:], xt_rows[:, r, :])
+        nc.sync.dma_start(w_words[:].bitcast(I32), wc_words[0].bitcast(I32))
+        for q in range(4):
+            nc.sync.dma_start(w_scales[32 * q : 32 * q + 4, :].bitcast(I32), wc_scales[0, 4 * q : 4 * q + 4, :].bitcast(I32))
+
+        picked = sb.tile([P, 2, J], BF16, name="picked")
+        picked_hi = sb.tile([P, 2, J], BF16, name="picked_hi")
+        for r in range(PACK):
+            dst = picked[:, r, :] if r < 2 else picked_hi[:, r - 2, :]
+            nc.vector.tensor_copy(dst, rows[r][:].indirect(offsets[:]))
+
+        dealt = picked[:].rearrange("p r (m t) -> p t m r", t=PACK)
+        dealt_hi = picked_hi[:].rearrange("p r (m t) -> p t m r", t=PACK)
+        x_in = [sb.tile([P, P, PACK], BF16, name=f"x_in{t}", align_bytes=64) for t in range(PACK)]
+        x_codes = [sb.tile([P, P], U32, name=f"x_codes{t}", align_bytes=64) for t in range(PACK)]
+        x_scales = [sb.tile([P, P], U8, name=f"x_scales{t}", align_bytes=64) for t in range(PACK)]
+        logits = [ps.tile([P, C], F32, name=f"logits{t}") for t in range(PACK)]
+        neg_max = [sb.tile([P, 1], F32, name=f"neg_max{t}") for t in range(PACK)]
+        total = sb.tile([P, PACK], F32, name="total")
+        inv = sb.tile([P, PACK], F32, name="inv")
+        e = [sb.tile([P, C], F32, name=f"e{t}") for t in range(PACK)]
+        y = sb.tile([P, PACK, C], F32, name="y")
+        out_rows = out_0.rearrange("(p t) c -> p t c", t=PACK)
+
+        def weave_x(t):
+            if t < 2:
+                nc.vector.tensor_copy(x_in[t][:, :, 2:4], dealt_hi[:, t])
+            else:
+                nc.scalar.copy(x_in[t][:, :, 2:4], dealt_hi[:, t])
+
+        def product(t):
+            nc.vector.quantize_mx(
+                out=x_codes[t][:].bitcast(FP8X4),
+                scales=x_scales[t][:],
+                in_=x_in[t][:].rearrange("p m r -> p (m r)"),
+            )
+            nc.tensor.matmul_mx(
+                out=logits[t][:],
+                lhsT=x_codes[t][:].bitcast(FP8X4),
+                lhsT_scale=x_scales[t][:],
+                rhs=w_words[:].bitcast(FP4X4),
+                rhs_scale=w_scales[:],
+                start=True,
+                stop=True,
+            )
+
+        def exps(t):
+            nc.vector.tensor_reduce(neg_max[t][:], logits[t][:], AX, ALU.max, negate=True)
+            nc.scalar.activation(e[t][:], logits[t][:], EXP, bias=neg_max[t][:], accum_out=total[:, t : t + 1])
+
+        def invert(a, b):
+            nc.vector.reciprocal(inv[:, a:b], total[:, a:b])
+
+        def shares(t, a, b):
+            nc.vector.tensor_scalar(y[:, t, a:b], e[t][:, a:b], inv[:, t : t + 1], 256.0, ALU.mult, ALU.mult)
+
+        def store(t):
+            nc.sync.dma_start(out_rows[:, t, :], y[:, t, :])
+
+        for t in range(PACK):
+            nc.scalar.copy(x_in[t][:, :, 0:2], dealt[:, t])
+        for t in range(PACK):
+            weave_x(t)
+        for t in range(PACK):
+            product(t)
+        for t in range(PACK):
+            exps(t)
+        invert(0, 2)
+        invert(2, 3)
+        for t in range(2):
+            shares(t, 0, C)
+            store(t)
+        invert(3, 4)
+        shares(2, 0, C)
+        store(2)
+        shares(3, 0, 256)
+        shares(3, 256, C)
+        store(3)
+
+        y_codes = sb.tile([P, C], U32, name="y_codes", align_bytes=64)
+        y_scales = sb.tile([P, C], U8, name="y_scales", align_bytes=64)
+        woven = y[:].rearrange("p t c -> p c t")
+        y_in = [sb.tile([P, 256, PACK], BF16, name=f"y_in{h}", align_bytes=64) for h in range(2)]
+        nc.vector.tensor_copy(y_in[0][:], woven[:, 0:256, :])
+        nc.vector.tensor_copy(y_in[1][:, 0:64, :], woven[:, 256:320, :])
+        nc.scalar.copy(y_in[1][:, 64:256, :], woven[:, 320:512, :])
+        words_out = out_1[0].rearrange("p c r -> p (c r)").bitcast(I32)
+        for h in range(2):
+            a, b = 256 * h, 256 * (h + 1)
+            nc.vector.quantize_mx(
+                out=y_codes[:, a:b].bitcast(FP8X4),
+                scales=y_scales[:, a:b],
+                in_=y_in[h][:].rearrange("p c t -> p (c t)"),
+            )
+            nc.sync.dma_start(words_out[:, a:b], y_codes[:, a:b].bitcast(I32))
+        for q in range(4):
+            eng = nc.scalar if q < 3 else nc.sync
+            eng.dma_start(out_2[0, 4 * q : 4 * q + 4, :].bitcast(I32), y_scales[32 * q : 32 * q + 4, :].bitcast(I32))

@@ -34,8 +34,8 @@ def tile_moe_expert_heads_to_classes_pl_kernel(tc, xt, wc_words, wc_scales, offs
         warm_in = sb.tile([P, 1], F32, name="warm_in")
         warm_out = sb.tile([P, 1], F32, name="warm_out")
 
-        nc.gpsimd.memset(warm_in[:], 0.0)
-        nc.gpsimd.memset(w_scales[:].bitcast(I32), 0)
+        nc.vector.memset(w_scales[:].bitcast(I32), 0)
+        nc.vector.memset(warm_in[:], 0.0)
         nc.scalar.activation(warm_out[:], warm_in[:], EXP)
 
         xt_rows = xt.rearrange("(p r) t -> p r t", r=PACK)
@@ -45,7 +45,7 @@ def tile_moe_expert_heads_to_classes_pl_kernel(tc, xt, wc_words, wc_scales, offs
             nc.sync.dma_start(rows[r][:], xt_rows[:, r, :])
         nc.sync.dma_start(w_words[:].bitcast(I32), wc_words[0].bitcast(I32))
         for q in range(4):
-            nc.sync.dma_start(w_scales[32 * q : 32 * q + 4, :].bitcast(I32), wc_scales[0, 4 * q : 4 * q + 4, :].bitcast(I32))
+            nc.scalar.dma_start(w_scales[32 * q : 32 * q + 4, :].bitcast(I32), wc_scales[0, 4 * q : 4 * q + 4, :].bitcast(I32))
 
         picked = sb.tile([P, 2, J], BF16, name="picked")
         picked_hi = sb.tile([P, 2, J], BF16, name="picked_hi")

@@ -15,10 +15,16 @@ FP8X4 = mybir.dt.float8_e4m3fn_x4
 FP4X4 = mybir.dt.float4_e2m1fn_x4
 ALU = mybir.AluOpType
 EXP = mybir.ActivationFunctionType.Exp
-AX = mybir.AxisListType.X
+FREE_AXIS = mybir.AxisListType.X
 
 P = 128
 PACK = 4
+GROUP = 16
+QUADRANTS = 4
+LAST = PACK - 1
+FIRST_PAIR, SECOND_PAIR = slice(0, 2), slice(2, 4)
+HALF = C // 2
+PART = C // 4
 
 
 def tile_moe_expert_heads_to_classes_pl_kernel(tc, xt, wc_words, wc_scales, offs, out_0, out_1, out_2):
@@ -27,16 +33,12 @@ def tile_moe_expert_heads_to_classes_pl_kernel(tc, xt, wc_words, wc_scales, offs
         sb = ctx.enter_context(tc.tile_pool(name="sb", bufs=1))
         ps = ctx.enter_context(tc.psum_pool(name="ps", bufs=1))
 
-        offsets = sb.tile([P, J // 16], U16, name="offsets")
+        offsets = sb.tile([P, J // GROUP], U16, name="offsets")
         rows = [sb.tile([P, T], F32, name=f"rows{r}") for r in range(PACK)]
         w_words = sb.tile([P, 2 * C], U8, name="w_words", align_bytes=64)
         w_scales = sb.tile([P, C], U8, name="w_scales", align_bytes=64)
-        warm_in = sb.tile([P, 1], F32, name="warm_in")
-        warm_out = sb.tile([P, 1], F32, name="warm_out")
 
         nc.vector.memset(w_scales[:].bitcast(I32), 0)
-        nc.vector.memset(warm_in[:], 0.0)
-        nc.scalar.activation(warm_out[:], warm_in[:], EXP)
 
         xt_rows = xt.rearrange("(p r) t -> p r t", r=PACK)
         nc.sync.dma_start(rows[0][:], xt_rows[:, 0, :])
@@ -44,17 +46,23 @@ def tile_moe_expert_heads_to_classes_pl_kernel(tc, xt, wc_words, wc_scales, offs
         for r in range(1, PACK):
             nc.sync.dma_start(rows[r][:], xt_rows[:, r, :])
         nc.sync.dma_start(w_words[:].bitcast(I32), wc_words[0].bitcast(I32))
-        for q in range(4):
-            nc.scalar.dma_start(w_scales[32 * q : 32 * q + 4, :].bitcast(I32), wc_scales[0, 4 * q : 4 * q + 4, :].bitcast(I32))
+        for q in range(QUADRANTS):
+            nc.scalar.dma_start(
+                w_scales[32 * q : 32 * q + 4, :].bitcast(I32),
+                wc_scales[0, 4 * q : 4 * q + 4, :].bitcast(I32),
+            )
 
-        picked = sb.tile([P, 2, J], BF16, name="picked")
-        picked_hi = sb.tile([P, 2, J], BF16, name="picked_hi")
-        for r in range(PACK):
-            dst = picked[:, r, :] if r < 2 else picked_hi[:, r - 2, :]
-            nc.vector.tensor_copy(dst, rows[r][:].indirect(offsets[:]))
+        picked = [sb.tile([P, 2, J], BF16, name=f"picked{pair}") for pair in range(2)]
+        for r in range(LAST):
+            nc.vector.tensor_copy(picked[r // 2][:, r % 2, :], rows[r][:].indirect(offsets[:]))
+        for first in (0, J // 2):
+            end = first + J // 2
+            nc.vector.tensor_copy(
+                picked[1][:, 1, first:end],
+                rows[LAST][:].indirect(offsets[:, first // GROUP : end // GROUP]),
+            )
+        dealt = [pair[:].rearrange("p r (m t) -> p t m r", t=PACK) for pair in picked]
 
-        dealt = picked[:].rearrange("p r (m t) -> p t m r", t=PACK)
-        dealt_hi = picked_hi[:].rearrange("p r (m t) -> p t m r", t=PACK)
         x_in = [sb.tile([P, P, PACK], BF16, name=f"x_in{t}", align_bytes=64) for t in range(PACK)]
         x_codes = [sb.tile([P, P], U32, name=f"x_codes{t}", align_bytes=64) for t in range(PACK)]
         x_scales = [sb.tile([P, P], U8, name=f"x_scales{t}", align_bytes=64) for t in range(PACK)]
@@ -66,13 +74,17 @@ def tile_moe_expert_heads_to_classes_pl_kernel(tc, xt, wc_words, wc_scales, offs
         y = sb.tile([P, PACK, C], F32, name="y")
         out_rows = out_0.rearrange("(p t) c -> p t c", t=PACK)
 
-        def weave_x(t):
-            if t < 2:
-                nc.vector.tensor_copy(x_in[t][:, :, 2:4], dealt_hi[:, t])
-            else:
-                nc.scalar.copy(x_in[t][:, :, 2:4], dealt_hi[:, t])
+        early, late = slice(0, P // 2), slice(P // 2, P)
+        for t in range(PACK):
+            nc.scalar.copy(x_in[t][:, :, FIRST_PAIR], dealt[0][:, t])
+        nc.scalar.copy(x_in[0][:, early, SECOND_PAIR], dealt[1][:, 0, early])
+        nc.scalar.copy(x_in[1][:, early, SECOND_PAIR], dealt[1][:, 1, early])
+        nc.scalar.copy(x_in[0][:, late, SECOND_PAIR], dealt[1][:, 0, late])
+        nc.vector.tensor_copy(x_in[1][:, late, SECOND_PAIR], dealt[1][:, 1, late])
+        for t in range(2, PACK):
+            nc.scalar.copy(x_in[t][:, :, SECOND_PAIR], dealt[1][:, t])
 
-        def product(t):
+        for t in range(PACK):
             nc.vector.quantize_mx(
                 out=x_codes[t][:].bitcast(FP8X4),
                 scales=x_scales[t][:],
@@ -88,55 +100,67 @@ def tile_moe_expert_heads_to_classes_pl_kernel(tc, xt, wc_words, wc_scales, offs
                 stop=True,
             )
 
-        def exps(t):
-            nc.vector.tensor_reduce(neg_max[t][:], logits[t][:], AX, ALU.max, negate=True)
+        def exponentials(t):
+            nc.vector.tensor_reduce(neg_max[t][:], logits[t][:], FREE_AXIS, ALU.max, negate=True)
             nc.scalar.activation(e[t][:], logits[t][:], EXP, bias=neg_max[t][:], accum_out=total[:, t : t + 1])
 
-        def invert(a, b):
-            nc.vector.reciprocal(inv[:, a:b], total[:, a:b])
+        def invert(t):
+            nc.vector.reciprocal(inv[:, t : t + 1], total[:, t : t + 1])
 
-        def shares(t, a, b):
-            nc.vector.tensor_scalar(y[:, t, a:b], e[t][:, a:b], inv[:, t : t + 1], 256.0, ALU.mult, ALU.mult)
+        def shares(t, first, end):
+            nc.vector.tensor_scalar(
+                y[:, t, first:end], e[t][:, first:end], inv[:, t : t + 1], 256.0, ALU.mult, ALU.mult
+            )
 
-        def store(t):
+        def store_shares(t):
             nc.sync.dma_start(out_rows[:, t, :], y[:, t, :])
-
-        for t in range(PACK):
-            nc.scalar.copy(x_in[t][:, :, 0:2], dealt[:, t])
-        for t in range(PACK):
-            weave_x(t)
-        for t in range(PACK):
-            product(t)
-        for t in range(PACK):
-            exps(t)
-        invert(0, 2)
-        invert(2, 3)
-        for t in range(2):
-            shares(t, 0, C)
-            store(t)
-        invert(3, 4)
-        shares(2, 0, C)
-        store(2)
-        shares(3, 0, 256)
-        shares(3, 256, C)
-        store(3)
 
         y_codes = sb.tile([P, C], U32, name="y_codes", align_bytes=64)
         y_scales = sb.tile([P, C], U8, name="y_scales", align_bytes=64)
-        woven = y[:].rearrange("p t c -> p c t")
-        y_in = [sb.tile([P, 256, PACK], BF16, name=f"y_in{h}", align_bytes=64) for h in range(2)]
-        nc.vector.tensor_copy(y_in[0][:], woven[:, 0:256, :])
-        nc.vector.tensor_copy(y_in[1][:, 0:64, :], woven[:, 256:320, :])
-        nc.scalar.copy(y_in[1][:, 64:256, :], woven[:, 320:512, :])
-        words_out = out_1[0].rearrange("p c r -> p (c r)").bitcast(I32)
-        for h in range(2):
-            a, b = 256 * h, 256 * (h + 1)
-            nc.vector.quantize_mx(
-                out=y_codes[:, a:b].bitcast(FP8X4),
-                scales=y_scales[:, a:b],
-                in_=y_in[h][:].rearrange("p c t -> p (c t)"),
+        y_in_scalar = sb.tile([P, HALF, PACK], BF16, name="y_in_scalar", align_bytes=64)
+        y_in_vector = [sb.tile([P, PART, PACK], BF16, name=f"y_in_vector{i}", align_bytes=64) for i in range(2)]
+        y_in = [y_in_vector[0][:], y_in_vector[1][:], y_in_scalar[:, :PART, :], y_in_scalar[:, PART:, :]]
+        by_class = y[:].rearrange("p t c -> p c t")
+
+        for t in range(LAST):
+            exponentials(t)
+        invert(0)
+        exponentials(LAST)
+        for t in range(LAST):
+            if t == 2:
+                nc.scalar.copy(y_in_scalar[:, :, FIRST_PAIR], by_class[:, HALF:, FIRST_PAIR])
+            invert(t + 1)
+            shares(t, 0, C)
+            store_shares(t)
+        shares(LAST, 0, HALF)
+        shares(LAST, HALF, C)
+        store_shares(LAST)
+
+        for i in range(2):
+            nc.vector.tensor_copy(
+                y_in[i].rearrange("p (c n) t -> p c t n", n=4),
+                y[:, :, i * PART : (i + 1) * PART].rearrange("p t (c n) -> p c t n", n=4),
             )
-            nc.sync.dma_start(words_out[:, a:b], y_codes[:, a:b].bitcast(I32))
-        for q in range(4):
-            eng = nc.scalar if q < 3 else nc.sync
-            eng.dma_start(out_2[0, 4 * q : 4 * q + 4, :].bitcast(I32), y_scales[32 * q : 32 * q + 4, :].bitcast(I32))
+        for i in range(2, 4):
+            nc.scalar.copy(y_in[i][:, :, SECOND_PAIR], by_class[:, i * PART : (i + 1) * PART, SECOND_PAIR])
+
+        def quantise_part(i):
+            classes = slice(i * PART, (i + 1) * PART)
+            nc.vector.quantize_mx(
+                out=y_codes[:, classes].bitcast(FP8X4),
+                scales=y_scales[:, classes],
+                in_=y_in[i].rearrange("p c t -> p (c t)"),
+            )
+
+        words_out = out_1[0].rearrange("p c r -> p (c r)").bitcast(I32)
+        for i in (0, 2, 1):
+            quantise_part(i)
+        nc.sync.dma_start(words_out[:, : 3 * PART], y_codes[:, : 3 * PART].bitcast(I32))
+        quantise_part(3)
+        nc.sync.dma_start(words_out[:, 3 * PART :], y_codes[:, 3 * PART :].bitcast(I32))
+        for q in range(QUADRANTS):
+            queue = nc.sync if q == QUADRANTS - 1 else nc.scalar
+            queue.dma_start(
+                out_2[0, 4 * q : 4 * q + 4, :].bitcast(I32),
+                y_scales[32 * q : 32 * q + 4, :].bitcast(I32),
+            )

from contextlib import ExitStack

import concourse.mybir as mybir

K, T, J, C = 512, 1024, 512, 512
FLOPS = 2 * J * K * C

F32 = mybir.dt.float32
BF16 = mybir.dt.bfloat16
I32 = mybir.dt.int32
U32 = mybir.dt.uint32
U16 = mybir.dt.uint16
U8 = mybir.dt.uint8
FP8X4 = mybir.dt.float8_e4m3fn_x4
FP4X4 = mybir.dt.float4_e2m1fn_x4
ALU = mybir.AluOpType
EXP = mybir.ActivationFunctionType.Exp
FREE_AXIS = mybir.AxisListType.X

P = 128
PACK = 4
GROUP = 16
QUADRANTS = 4
LAST = PACK - 1
FIRST_PAIR, SECOND_PAIR = slice(0, 2), slice(2, 4)
HALF = C // 2
PART = C // 4


def tile_moe_expert_heads_to_classes_pl_kernel(tc, xt, wc_words, wc_scales, offs, out_0, out_1, out_2):
    nc = tc.nc
    with ExitStack() as ctx:
        sb = ctx.enter_context(tc.tile_pool(name="sb", bufs=1))
        ps = ctx.enter_context(tc.psum_pool(name="ps", bufs=1))

        offsets = sb.tile([P, J // GROUP], U16, name="offsets")
        rows = [sb.tile([P, T], F32, name=f"rows{r}") for r in range(PACK)]
        w_words = sb.tile([P, 2 * C], U8, name="w_words", align_bytes=64)
        w_scales = sb.tile([P, C], U8, name="w_scales", align_bytes=64)

        nc.vector.memset(w_scales[:].bitcast(I32), 0)

        xt_rows = xt.rearrange("(p r) t -> p r t", r=PACK)
        nc.sync.dma_start(rows[0][:], xt_rows[:, 0, :])
        nc.sync.dma_start(offsets[:], offs)
        for r in range(1, PACK):
            nc.sync.dma_start(rows[r][:], xt_rows[:, r, :])
        nc.sync.dma_start(w_words[:].bitcast(I32), wc_words[0].bitcast(I32))
        for q in range(QUADRANTS):
            nc.scalar.dma_start(
                w_scales[32 * q : 32 * q + 4, :].bitcast(I32),
                wc_scales[0, 4 * q : 4 * q + 4, :].bitcast(I32),
            )

        picked = [sb.tile([P, 2, J], BF16, name=f"picked{pair}") for pair in range(2)]
        for r in range(LAST):
            nc.vector.tensor_copy(picked[r // 2][:, r % 2, :], rows[r][:].indirect(offsets[:]))
        for first in (0, J // 2):
            end = first + J // 2
            nc.vector.tensor_copy(
                picked[1][:, 1, first:end],
                rows[LAST][:].indirect(offsets[:, first // GROUP : end // GROUP]),
            )
        dealt = [pair[:].rearrange("p r (m t) -> p t m r", t=PACK) for pair in picked]

        x_in = [sb.tile([P, P, PACK], BF16, name=f"x_in{t}", align_bytes=64) for t in range(PACK)]
        x_codes = [sb.tile([P, P], U32, name=f"x_codes{t}", align_bytes=64) for t in range(PACK)]
        x_scales = [sb.tile([P, P], U8, name=f"x_scales{t}", align_bytes=64) for t in range(PACK)]
        logits = [ps.tile([P, C], F32, name=f"logits{t}") for t in range(PACK)]
        neg_max = [sb.tile([P, 1], F32, name=f"neg_max{t}") for t in range(PACK)]
        total = sb.tile([P, PACK], F32, name="total")
        inv = sb.tile([P, PACK], F32, name="inv")
        e = [sb.tile([P, C], F32, name=f"e{t}") for t in range(PACK)]
        y = sb.tile([P, PACK, C], F32, name="y")
        out_rows = out_0.rearrange("(p t) c -> p t c", t=PACK)

        early, late = slice(0, P // 2), slice(P // 2, P)
        for t in range(PACK):
            nc.scalar.copy(x_in[t][:, :, FIRST_PAIR], dealt[0][:, t])
        nc.scalar.copy(x_in[0][:, early, SECOND_PAIR], dealt[1][:, 0, early])
        nc.scalar.copy(x_in[1][:, early, SECOND_PAIR], dealt[1][:, 1, early])
        nc.scalar.copy(x_in[0][:, late, SECOND_PAIR], dealt[1][:, 0, late])
        nc.vector.tensor_copy(x_in[1][:, late, SECOND_PAIR], dealt[1][:, 1, late])
        for t in range(2, PACK):
            nc.scalar.copy(x_in[t][:, :, SECOND_PAIR], dealt[1][:, t])

        for t in range(PACK):
            nc.vector.quantize_mx(
                out=x_codes[t][:].bitcast(FP8X4),
                scales=x_scales[t][:],
                in_=x_in[t][:].rearrange("p m r -> p (m r)"),
            )
            nc.tensor.matmul_mx(
                out=logits[t][:],
                lhsT=x_codes[t][:].bitcast(FP8X4),
                lhsT_scale=x_scales[t][:],
                rhs=w_words[:].bitcast(FP4X4),
                rhs_scale=w_scales[:],
                start=True,
                stop=True,
            )

        def exponentials(t):
            nc.vector.tensor_reduce(neg_max[t][:], logits[t][:], FREE_AXIS, ALU.max, negate=True)
            nc.scalar.activation(e[t][:], logits[t][:], EXP, bias=neg_max[t][:], accum_out=total[:, t : t + 1])

        def invert(t):
            nc.vector.reciprocal(inv[:, t : t + 1], total[:, t : t + 1])

        def shares(t, first, end):
            nc.vector.tensor_scalar(
                y[:, t, first:end], e[t][:, first:end], inv[:, t : t + 1], 256.0, ALU.mult, ALU.mult
            )

        def store_shares(t):
            nc.sync.dma_start(out_rows[:, t, :], y[:, t, :])

        y_codes = sb.tile([P, C], U32, name="y_codes", align_bytes=64)
        y_scales = sb.tile([P, C], U8, name="y_scales", align_bytes=64)
        y_in_scalar = sb.tile([P, HALF, PACK], BF16, name="y_in_scalar", align_bytes=64)
        y_in_vector = [sb.tile([P, PART, PACK], BF16, name=f"y_in_vector{i}", align_bytes=64) for i in range(2)]
        y_in = [y_in_vector[0][:], y_in_vector[1][:], y_in_scalar[:, :PART, :], y_in_scalar[:, PART:, :]]
        by_class = y[:].rearrange("p t c -> p c t")

        for t in range(LAST):
            exponentials(t)
        invert(0)
        exponentials(LAST)
        for t in range(LAST):
            if t == 2:
                nc.scalar.copy(y_in_scalar[:, :, FIRST_PAIR], by_class[:, HALF:, FIRST_PAIR])
            invert(t + 1)
            shares(t, 0, C)
            store_shares(t)
        shares(LAST, 0, HALF)
        shares(LAST, HALF, C)
        store_shares(LAST)

        for i in range(2):
            nc.vector.tensor_copy(
                y_in[i].rearrange("p (c n) t -> p c t n", n=4),
                y[:, :, i * PART : (i + 1) * PART].rearrange("p t (c n) -> p c t n", n=4),
            )
        for i in range(2, 4):
            nc.scalar.copy(y_in[i][:, :, SECOND_PAIR], by_class[:, i * PART : (i + 1) * PART, SECOND_PAIR])

        def quantise_part(i):
            classes = slice(i * PART, (i + 1) * PART)
            nc.vector.quantize_mx(
                out=y_codes[:, classes].bitcast(FP8X4),
                scales=y_scales[:, classes],
                in_=y_in[i].rearrange("p c t -> p (c t)"),
            )

        words_out = out_1[0].rearrange("p c r -> p (c r)").bitcast(I32)
        for i in (0, 2, 1):
            quantise_part(i)
        nc.sync.dma_start(words_out[:, : 3 * PART], y_codes[:, : 3 * PART].bitcast(I32))
        quantise_part(3)
        nc.sync.dma_start(words_out[:, 3 * PART :], y_codes[:, 3 * PART :].bitcast(I32))
        for q in range(QUADRANTS):
            queue = nc.sync if q == QUADRANTS - 1 else nc.scalar
            queue.dma_start(
                out_2[0, 4 * q : 4 * q + 4, :].bitcast(I32),
                y_scales[32 * q : 32 * q + 4, :].bitcast(I32),
            )
